import numpy as np
import ml_dtypes


def mxq(x, axis, fmt="e4m3"):
    dtype, down = {"e4m3": (ml_dtypes.float8_e4m3fn, 7), "e5m2": (ml_dtypes.float8_e5m2, 14)}[fmt]
    v = np.moveaxis(np.asarray(x, np.float32).astype(ml_dtypes.bfloat16).astype(np.float64), axis, -1)
    blocks = v.reshape(v.shape[:-1] + (-1, 32))
    amax = np.abs(blocks).max(-1, keepdims=True)
    byte = np.maximum(np.where(amax > 0, np.frexp(amax)[1] - 1 + 127, 0) - down, 1)
    scale = np.exp2(byte - 127.0)
    codes = (blocks / scale).astype(np.float32).astype(dtype).astype(np.float64)
    return np.moveaxis((codes * scale).reshape(v.shape), -1, axis)


WIDE = False


def mx_kscale(k):
    if not WIDE:
        return np.ones(k)
    levels = np.array([30, -30])
    if k % 512:
        return np.exp2(np.random.permutation(np.resize(levels, k // 32))).repeat(32)
    a = np.empty((k // 512, 16))
    for p in range(k // 512):
        a[p, :8] = np.random.permutation(np.resize(levels, 8))
        for g in range(8):
            far = levels[np.abs(levels - a[p, g]) >= 10]
            a[p, g + 8] = far[np.random.randint(len(far))]
    return np.exp2(a.ravel()).repeat(32)


BF16 = ml_dtypes.bfloat16


def bf(x):
    return np.asarray(x, np.float32).astype(BF16)


def f64(x):
    return np.asarray(x).astype(np.float64)


E2M1 = np.array([0.0, 0.5, 1.0, 1.5, 2.0, 3.0, 4.0, 6.0, -0.0, -0.5, -1.0, -1.5, -2.0, -3.0, -4.0, -6.0])


def pack_weight(w, fmt):
    k, n = w.shape
    w = f64(bf(w)).reshape(k // 32, 32, n)
    amax = np.abs(w).max(1)
    if fmt == "e4m3":
        byte = np.frexp(amax)[1] - 1 + 127 - 7
    else:
        mant, ex = np.frexp(amax / 6.0)
        byte = np.where(mant > 0.5, ex, ex - 1) + 127
    byte = np.clip(np.where(amax > 0, byte, 1), 1, 254)
    scaled = (w * np.exp2(127.0 - byte)[:, None, :]).reshape(k, n).astype(np.float32)
    by_word = np.ascontiguousarray(scaled.reshape(k // 512, 128, 4, n).transpose(0, 1, 3, 2))
    if fmt == "e4m3":
        words = by_word.astype(ml_dtypes.float8_e4m3fn).view(np.uint8)
    else:
        c = by_word.astype(ml_dtypes.float4_e2m1fn).view(np.uint8) & 0xF
        words = c[..., 0::2] | (c[..., 1::2] << 4)
    return np.ascontiguousarray(words), np.ascontiguousarray(byte.astype(np.uint8).reshape(k // 512, 16, n))


def unpack_weight(words, scales, fmt):
    g, p, n, _ = words.shape
    if fmt == "e4m3":
        vals = np.ascontiguousarray(words).view(ml_dtypes.float8_e4m3fn).astype(np.float64)
    else:
        nib = np.empty((g, p, n, 4), np.uint8)
        nib[..., 0::2] = words & 0xF
        nib[..., 1::2] = words >> 4
        vals = E2M1[nib]
    vals = vals * np.repeat(np.exp2(scales.astype(np.float64) - 127.0), 8, axis=1)[..., None]
    return vals.transpose(0, 1, 3, 2).reshape(g * 512, n)
def pack4(w):
    words, scales = pack_weight(w, "e2m1")
    return words.reshape(words.shape[0], 128, -1), scales


def unpack4(words, scales):
    return unpack_weight(words.reshape(words.shape[0], 128, -1, 2), scales, "e2m1")


M, K, N = 1024, 2048, 1024


def setup_inputs():
    s = mx_kscale(K)
    t = mx_kscale(N)
    y = bf(np.random.standard_normal((M, K)) * s)
    pinv = np.random.standard_normal((K, N)) / np.sqrt(K) / s[:, None]
    pinv_words, pinv_scales = pack4(pinv)
    u = bf(0.7 * np.random.standard_normal((M, N)))
    window = bf((1 + 0.1 * np.random.standard_normal(N)) * t)
    qfilter = bf(np.random.standard_normal((N, N)) / np.sqrt(N) / t[:, None])
    command = bf(np.random.standard_normal((M, N)))
    limit = bf(1.5 + 0.1 * np.random.standard_normal(N))
    return {"y": y, "pinv_words": pinv_words, "pinv_scales": pinv_scales, "u": u,
            "window": window, "qfilter": qfilter, "command": command, "limit": limit}


def reference(y, pinv_words, pinv_scales, u, window, qfilter, command, limit):
    h = mxq(f64(y), 1, "e4m3") @ unpack4(pinv_words, pinv_scales)
    e = (h - f64(u)) * f64(window)
    d = mxq(e, 1, "e5m2") @ mxq(f64(qfilter), 0, "e4m3")
    lim = f64(limit)
    v = np.maximum(np.minimum(f64(command) - d, lim), -lim)
    return d, v

@@ -1,0 +1,381 @@
+from contextlib import ExitStack
+
+import concourse.mybir as mybir
+from concourse.masks import make_identity
+
+M, K, N = 1024, 2048, 1024
+FLOPS = 2 * M * K * N + 2 * M * N * N
+
+F32 = mybir.dt.float32
+BF16 = mybir.dt.bfloat16
+I32 = mybir.dt.int32
+U32 = mybir.dt.uint32
+U8 = mybir.dt.uint8
+E4M3 = mybir.dt.float8_e4m3fn_x4
+E5M2 = mybir.dt.float8_e5m2_x4
+E2M1 = mybir.dt.float4_e2m1fn_x4
+ADD = mybir.AluOpType.add
+SUB = mybir.AluOpType.subtract
+MUL = mybir.AluOpType.mult
+MIN = mybir.AluOpType.min
+MAX = mybir.AluOpType.max
+COPY = mybir.ActivationFunctionType.Copy
+
+P = 128
+PACK = 4
+KG = K // 512
+NG = N // 512
+TILES = M // P
+HALF = 512
+LAG = 2
+QE = "SVSV"
+GCOLS = 768
+GFILL = 0
+
+
+def tile_lifted_disturbance_observer_s9_kernel(
+    tc, y, pinv_words, pinv_scales, u, window, qfilter, command, limit, out_0, out_1
+):
+    nc = tc.nc
+    with ExitStack() as ctx:
+        keep = ctx.enter_context(tc.tile_pool(name="keep", bufs=1))
+        rows = ctx.enter_context(tc.tile_pool(name="rows", bufs=TILES))
+        work = ctx.enter_context(tc.tile_pool(name="work", bufs=3))
+        deep = ctx.enter_context(tc.tile_pool(name="deep", bufs=3))
+        ps_y = ctx.enter_context(tc.psum_pool(name="ps_y", bufs=2))
+        ps_e = ctx.enter_context(tc.psum_pool(name="ps_e", bufs=1))
+        ps_h = ctx.enter_context(tc.psum_pool(name="ps_h", bufs=2))
+        ps_d = ctx.enter_context(tc.psum_pool(name="ps_d", bufs=3))
+
+        ident = keep.tile([P, P], F32, name="ident")
+        ident_b = keep.tile([P, P], BF16, name="ident_b")
+        vec = keep.tile([P, P], BF16, name="vec")
+        vcol = keep.tile([P, 16], BF16, name="vcol")
+        wb = keep.tile([P, N], BF16, name="wb")
+        lb = keep.tile([P, N], BF16, name="lb")
+        pw = [keep.tile([P, KG, N], U8, name="pw%d" % n, align_bytes=64) for n in range(2)]
+        pscale = keep.tile([P, KG, N], U8, name="pscale", align_bytes=64)
+        q_raw = keep.tile([P, NG, 2, PACK, HALF], BF16, name="q_raw")
+        q_grp = keep.tile([P, NG, 2, HALF, PACK], BF16, name="q_grp", align_bytes=64)
+        q_codes = keep.tile([P, NG, N], U32, name="q_codes", align_bytes=64)
+        q_scale = keep.tile([P, NG, N], U8, name="q_scale", align_bytes=64)
+
+        T = [dict() for i in range(TILES)]
+
+        def gcols(i):
+            return GFILL if i < 2 else GCOLS
+
+        def rsl(i):
+            return slice(i * P, (i + 1) * P)
+
+        def load_y(i, parts=1):
+            t = rows.tile([P, K], BF16, name="y_sb")
+            T[i]["y"] = t
+            w = K // parts
+            for j in range(parts):
+                nc.sync.dma_start(out=t[:, j * w : (j + 1) * w], in_=y[rsl(i), j * w : (j + 1) * w])
+
+        def load_u(i):
+            t = rows.tile([P, N], BF16, name="u_sb")
+            T[i]["u"] = t
+            nc.sync.dma_start(out=t[:], in_=u[rsl(i), :])
+
+        def load_c(i):
+            t = rows.tile([P, N], BF16, name="c_sb")
+            T[i]["c"] = t
+            nc.sync.dma_start(out=t[:], in_=command[rsl(i), :])
+
+        def load_q(g, n):
+            c = slice(n * HALF, (n + 1) * HALF)
+            nc.sync.dma_start(
+                out=q_raw[:, g, n, :, :],
+                in_=qfilter[g * 512 : (g + 1) * 512, c].rearrange("(p j) n -> p j n", j=PACK),
+            )
+
+        def turn_y(i):
+            words = T[i]["y"][:].bitcast(F32)
+            banks = []
+            for b in range(2):
+                bank = ps_y.tile([P, 2, 2, P], F32, name="yT", tag="yT")
+                for gg in range(2):
+                    g = 2 * b + gg
+                    for h in range(2):
+                        nc.tensor.transpose(
+                            bank[:, gg, h, :], words[:, 256 * g + h : 256 * (g + 1) : 2], ident[:]
+                        )
+                banks.append(bank)
+            T[i]["yT"] = banks
+
+        def group_y(i):
+            grp = work.tile([P, KG, P, PACK], BF16, name="y_grp", align_bytes=64)
+            T[i]["yg"] = grp
+            wv = grp[:].rearrange("p g m t -> p (g m t)").bitcast(F32)
+            for b in range(2):
+                nc.scalar.copy(
+                    out=wv[:, 512 * b : 512 * (b + 1)].rearrange("p (g m h) -> p g m h", g=2, h=2),
+                    in_=T[i]["yT"][b][:].rearrange("p g h m -> p g m h"),
+                )
+
+        def quant_y(i):
+            codes = deep.tile([P, KG * P], U32, name="y_codes", align_bytes=64)
+            scale = deep.tile([P, KG * P], U8, name="y_scale", align_bytes=64)
+            T[i]["yc"] = codes
+            T[i]["ys"] = scale
+            nc.vector.quantize_mx(
+                out=codes[:].bitcast(E4M3), scales=scale[:],
+                in_=T[i]["yg"][:].rearrange("p g m t -> p (g m t)"),
+            )
+
+        def mm1(i):
+            T[i]["h"] = []
+            for n in range(2):
+                acc = ps_h.tile([P, HALF], F32, name="h", tag="h")
+                T[i]["h"].append(acc)
+                for g in range(KG):
+                    nc.tensor.matmul_mx(
+                        out=acc[:],
+                        lhsT=T[i]["yc"][:, g * P : (g + 1) * P].bitcast(E4M3),
+                        lhsT_scale=T[i]["ys"][:, g * P : (g + 1) * P],
+                        rhs=pw[n][:, g, :].bitcast(E2M1),
+                        rhs_scale=pscale[:, g, n * HALF : (n + 1) * HALF],
+                        start=(g == 0),
+                        stop=(g == KG - 1),
+                    )
+
+        def sub_u(i):
+            r = work.tile([P, N], F32, name="r")
+            T[i]["r"] = r
+            e = work.tile([P, N], BF16, name="e")
+            T[i]["e"] = e
+            for n in range(2):
+                c = slice(n * HALF, (n + 1) * HALF)
+                nc.vector.tensor_tensor(out=r[:, c], in0=T[i]["h"][n][:], in1=T[i]["u"][:, c], op=SUB)
+                g = slice(n * HALF, min((n + 1) * HALF, gcols(i)))
+                if g.start < g.stop:
+                    nc.gpsimd.tensor_tensor(out=T[i]["e"][:, g], in0=r[:, g], in1=wb[:, g], op=MUL)
+
+        def mul_w_v(i):
+            for c0 in range(gcols(i), N, HALF):
+                c = slice(c0, min(c0 + HALF, N))
+                nc.vector.tensor_tensor(out=T[i]["e"][:, c], in0=T[i]["r"][:, c], in1=wb[:, c], op=MUL)
+
+        def turn_e(i):
+            words = T[i]["e"][:].bitcast(F32)
+            bank = ps_e.tile([P, NG, 2, P], F32, name="eT")
+            T[i]["eT"] = bank
+            for g in range(NG):
+                for h in range(2):
+                    nc.tensor.transpose(bank[:, g, h, :], words[:, 256 * g + h : 256 * (g + 1) : 2], ident[:])
+
+        def group_e(i):
+            grp = work.tile([P, NG, P, PACK], BF16, name="e_grp", align_bytes=64)
+            T[i]["eg"] = grp
+            wv = grp[:].rearrange("p g m t -> p (g m t)").bitcast(F32)
+            nc.scalar.copy(
+                out=wv.rearrange("p (g m h) -> p g m h", g=NG, h=2),
+                in_=T[i]["eT"][:].rearrange("p g h m -> p g m h"),
+            )
+
+        def quant_e(i):
+            codes = work.tile([P, NG * P], U32, name="e_codes", align_bytes=64)
+            scale = work.tile([P, NG * P], U8, name="e_scale", align_bytes=64)
+            T[i]["ec"] = codes
+            T[i]["es"] = scale
+            nc.vector.quantize_mx(
+                out=codes[:].bitcast(E5M2), scales=scale[:],
+                in_=T[i]["eg"][:].rearrange("p g m t -> p (g m t)"),
+            )
+
+        def mm2(i):
+            T[i]["d"] = []
+            for n in range(2):
+                acc = ps_d.tile([P, HALF], F32, name="d")
+                T[i]["d"].append(acc)
+                for g in range(NG):
+                    nc.tensor.matmul_mx(
+                        out=acc[:],
+                        lhsT=T[i]["ec"][:, g * P : (g + 1) * P].bitcast(E5M2),
+                        lhsT_scale=T[i]["es"][:, g * P : (g + 1) * P],
+                        rhs=q_codes[:, g, n * HALF : (n + 1) * HALF].bitcast(E4M3),
+                        rhs_scale=q_scale[:, g, n * HALF : (n + 1) * HALF],
+                        start=(g == 0),
+                        stop=(g == NG - 1),
+                    )
+
+        def copy_d(i):
+            t = deep.tile([P, N], F32, name="d_sb")
+            T[i]["ds"] = t
+            for n in range(2):
+                nc.scalar.copy(out=t[:, n * HALF : (n + 1) * HALF], in_=T[i]["d"][n][:])
+
+        def store_d(i):
+            nc.sync.dma_start(out=out_0[rsl(i), :], in_=T[i]["ds"][:])
+
+        def sub_d(i):
+            t = work.tile([P, N], F32, name="x")
+            T[i]["x"] = t
+            for n in range(2):
+                c = slice(n * HALF, (n + 1) * HALF)
+                nc.vector.tensor_tensor(out=t[:, c], in0=T[i]["c"][:, c], in1=T[i]["d"][n][:], op=SUB)
+
+        def cap(i, c):
+            nc.vector.tensor_tensor(out=T[i]["x"][:, c], in0=T[i]["x"][:, c], in1=lb[:, c], op=MIN)
+
+        def floor_(i, c):
+            if "v" not in T[i]:
+                t = deep.tile([P, N], F32, name="v")
+                T[i]["v"] = t
+            nc.vector.scalar_tensor_tensor(
+                out=T[i]["v"][:, c], in0=lb[:, c], scalar=-1.0, in1=T[i]["x"][:, c], op0=MUL, op1=MAX
+            )
+
+        def store_v(i, c):
+            nc.sync.dma_start(out=out_1[rsl(i), c], in_=T[i]["v"][:, c])
+
+        def group_q(n, g, eng):
+            src = q_raw[:, g, n, :, :].rearrange("p j c -> p c j")
+            if eng == "S":
+                nc.scalar.copy(out=q_grp[:, g, n, :, :], in_=src)
+            elif eng == "G":
+                nc.gpsimd.tensor_scalar(out=q_grp[:, g, n, :, :], in0=src, scalar1=1.0, scalar2=0.0, op0=MUL, op1=ADD)
+            else:
+                nc.vector.tensor_copy(out=q_grp[:, g, n, :, :], in_=src)
+
+        def quant_q(n, g):
+            c = slice(n * HALF, (n + 1) * HALF)
+            nc.vector.quantize_mx(
+                out=q_codes[:, g, c].bitcast(E4M3), scales=q_scale[:, g, c],
+                in_=q_grp[:, g, n, :, :].rearrange("p c j -> p (c j)"),
+            )
+
+        ALL = slice(0, N)
+
+        def load_p(n):
+            nc.sync.dma_start(
+                out=pw[n][:].bitcast(I32),
+                in_=pinv_words[:, :, n * N : (n + 1) * N].bitcast(I32).rearrange("g p n -> p g n"),
+            )
+
+        def load_s():
+            for Q in range(4):
+                nc.sync.dma_start(
+                    out=ps32[32 * Q : 32 * Q + 4, :].rearrange("q (g n) -> q g n", g=KG),
+                    in_=pinv_scales[:, 4 * Q : 4 * Q + 4, :].bitcast(I32).rearrange("g q n -> q g n"),
+                )
+
+        ps32 = pscale[:].rearrange("p g n -> p (g n)").bitcast(I32)
+        nc.vector.memset(vec[:], 0.0)
+        nc.vector.memset(ps32, 0)
+        make_identity(nc, ident[:])
+        make_identity(nc, ident_b[:])
+        load_y(0)
+        load_p(0)
+        load_s()
+        load_u(0)
+        load_p(1)
+        nc.scalar.dma_start(out=vec[0:8, :], in_=window.rearrange("(a b) -> a b", b=P))
+        nc.scalar.dma_start(out=vec[8:16, :], in_=limit.rearrange("(a b) -> a b", b=P))
+        load_y(1)
+        load_u(1)
+        load_q(0, 0)
+        load_q(1, 0)
+        load_q(0, 1)
+        load_q(1, 1)
+        load_y(2)
+        load_u(2)
+        load_c(0)
+        load_y(3)
+        load_u(3)
+        load_c(1)
+        load_y(4)
+        load_u(4)
+        load_c(2)
+        load_y(5)
+        load_u(5)
+        load_c(3)
+        load_y(6)
+        load_u(6)
+        load_c(4)
+        load_y(7)
+        load_u(7)
+        load_c(5)
+        load_c(6)
+        load_c(7)
+
+        turn_y(0)
+        group_y(0)
+        quant_y(0)
+        vT = ps_e.tile([P, P], BF16, name="vT", tag="eT")
+        nc.tensor.transpose(vT[:], vec[:], ident_b[:])
+        nc.scalar.copy(out=vcol[:], in_=vT[:, 0:16])
+        wB = ps_d.tile([P, N], BF16, name="wB", tag="d")
+        for j in range(8):
+            nc.tensor.transpose(wB[:, j * P : (j + 1) * P], vcol[:, j : j + 1].to_broadcast([P, P]), ident_b[:])
+        nc.scalar.copy(out=wb[:], in_=wB[:])
+        mm1(0)
+        turn_y(1)
+        group_y(1)
+        sub_u(0)
+        mul_w_v(0)
+        turn_e(0)
+        group_e(0)
+        quant_y(1)
+        mm1(1)
+        quant_e(0)
+        for n, g in ((0, 0), (0, 1), (1, 0), (1, 1)):
+            group_q(n, g, QE[2 * n + g])
+            quant_q(n, g)
+            if n == 0 and g == 1:
+                turn_y(2)
+                group_y(2)
+                sub_u(1)
+                mul_w_v(1)
+        mm2(0)
+        turn_e(1)
+        group_e(1)
+        quant_y(2)
+        mm1(2)
+        copy_d(0)
+        store_d(0)
+        lB = ps_d.tile([P, N], BF16, name="lB", tag="d")
+        for j in range(8):
+            nc.tensor.transpose(lB[:, j * P : (j + 1) * P], vcol[:, 8 + j : 9 + j].to_broadcast([P, P]), ident_b[:])
+        nc.scalar.copy(out=lb[:], in_=lB[:])
+        turn_y(3)
+        group_y(3)
+        quant_e(1)
+        EARLY = False
+        for s in range(2, TILES + 2):
+            i = s - 2
+            if s < TILES:
+                sub_u(s)
+            if s + 1 < TILES:
+                quant_y(s + 1)
+                mm1(s + 1)
+            if s - 1 < TILES:
+                mm2(s - 1)
+            if i > 0 or not EARLY:
+                sub_d(i)
+            if s < TILES:
+                mul_w_v(s)
+            if s - 1 < TILES:
+                copy_d(s - 1)
+                store_d(s - 1)
+            if s < TILES:
+                turn_e(s)
+                group_e(s)
+                quant_e(s)
+            if s + 2 < TILES:
+                turn_y(s + 2)
+                group_y(s + 2)
+            if i > 0 or not EARLY:
+                if i < TILES - 1:
+                    cap(i, ALL)
+                    floor_(i, ALL)
+                    store_v(i, ALL)
+                else:
+                    for c0 in range(0, N, 256):
+                        cap(i, slice(c0, c0 + 256))
+                    for c0 in range(0, N, 256):
+                        floor_(i, slice(c0, c0 + 256))
+                        store_v(i, slice(c0, c0 + 256))

@@ -27,10 +27,9 @@ KG = K // 512
 NG = N // 512
 TILES = M // P
 HALF = 512
-LAG = 2
-QE = "SVSV"
-GCOLS = 768
-GFILL = 0
+QE = ""
+GCOLS = 512
+GFILL = 512
 
 
 def tile_lifted_disturbance_observer_s9_kernel(
@@ -46,6 +45,7 @@ def tile_lifted_disturbance_observer_s9_kernel(
         ps_e = ctx.enter_context(tc.psum_pool(name="ps_e", bufs=1))
         ps_h = ctx.enter_context(tc.psum_pool(name="ps_h", bufs=2))
         ps_d = ctx.enter_context(tc.psum_pool(name="ps_d", bufs=3))
+        ctx.enter_context(tc.manual_schedule())
 
         ident = keep.tile([P, P], F32, name="ident")
         ident_b = keep.tile([P, P], BF16, name="ident_b")
@@ -53,9 +53,9 @@ def tile_lifted_disturbance_observer_s9_kernel(
         vcol = keep.tile([P, 16], BF16, name="vcol")
         wb = keep.tile([P, N], BF16, name="wb")
         lb = keep.tile([P, N], BF16, name="lb")
-        pw = [keep.tile([P, KG, N], U8, name="pw%d" % n, align_bytes=64) for n in range(2)]
+        pw = keep.tile([P, KG, 2 * N], U8, name="pw", align_bytes=64)
         pscale = keep.tile([P, KG, N], U8, name="pscale", align_bytes=64)
-        q_raw = keep.tile([P, NG, 2, PACK, HALF], BF16, name="q_raw")
+        q_raw = keep.tile([P, NG, PACK, N], BF16, name="q_raw")
         q_grp = keep.tile([P, NG, 2, HALF, PACK], BF16, name="q_grp", align_bytes=64)
         q_codes = keep.tile([P, NG, N], U32, name="q_codes", align_bytes=64)
         q_scale = keep.tile([P, NG, N], U8, name="q_scale", align_bytes=64)
@@ -85,36 +85,32 @@ def tile_lifted_disturbance_observer_s9_kernel(
             T[i]["c"] = t
             nc.sync.dma_start(out=t[:], in_=command[rsl(i), :])
 
-        def load_q(g, n):
-            c = slice(n * HALF, (n + 1) * HALF)
+        def load_q(g):
             nc.sync.dma_start(
-                out=q_raw[:, g, n, :, :],
-                in_=qfilter[g * 512 : (g + 1) * 512, c].rearrange("(p j) n -> p j n", j=PACK),
+                out=q_raw[:, g, :, :],
+                in_=qfilter[g * 512 : (g + 1) * 512, :].rearrange("(p j) n -> p j n", j=PACK),
             )
 
-        def turn_y(i):
+        def turn_y(i, b):
             words = T[i]["y"][:].bitcast(F32)
-            banks = []
-            for b in range(2):
-                bank = ps_y.tile([P, 2, 2, P], F32, name="yT", tag="yT")
-                for gg in range(2):
-                    g = 2 * b + gg
-                    for h in range(2):
-                        nc.tensor.transpose(
-                            bank[:, gg, h, :], words[:, 256 * g + h : 256 * (g + 1) : 2], ident[:]
-                        )
-                banks.append(bank)
-            T[i]["yT"] = banks
+            bank = ps_y.tile([P, 2, 2, P], F32, name="yT", tag="yT")
+            T[i]["yT", b] = bank
+            for gg in range(2):
+                g = 2 * b + gg
+                for h in range(2):
+                    nc.tensor.transpose(
+                        bank[:, gg, h, :], words[:, 256 * g + h : 256 * (g + 1) : 2], ident[:]
+                    )
 
-        def group_y(i):
-            grp = work.tile([P, KG, P, PACK], BF16, name="y_grp", align_bytes=64)
-            T[i]["yg"] = grp
-            wv = grp[:].rearrange("p g m t -> p (g m t)").bitcast(F32)
-            for b in range(2):
-                nc.scalar.copy(
-                    out=wv[:, 512 * b : 512 * (b + 1)].rearrange("p (g m h) -> p g m h", g=2, h=2),
-                    in_=T[i]["yT"][b][:].rearrange("p g h m -> p g m h"),
-                )
+        def group_y(i, b):
+            if b == 0:
+                grp = work.tile([P, KG, P, PACK], BF16, name="y_grp", align_bytes=64)
+                T[i]["yg"] = grp
+            wv = T[i]["yg"][:].rearrange("p g m t -> p (g m t)").bitcast(F32)
+            nc.scalar.copy(
+                out=wv[:, 512 * b : 512 * (b + 1)].rearrange("p (g m h) -> p g m h", g=2, h=2),
+                in_=T[i]["yT", b][:].rearrange("p g h m -> p g m h"),
+            )
 
         def quant_y(i):
             codes = deep.tile([P, KG * P], U32, name="y_codes", align_bytes=64)
@@ -126,37 +122,37 @@ def tile_lifted_disturbance_observer_s9_kernel(
                 in_=T[i]["yg"][:].rearrange("p g m t -> p (g m t)"),
             )
 
-        def mm1(i):
-            T[i]["h"] = []
-            for n in range(2):
-                acc = ps_h.tile([P, HALF], F32, name="h", tag="h")
-                T[i]["h"].append(acc)
-                for g in range(KG):
-                    nc.tensor.matmul_mx(
-                        out=acc[:],
-                        lhsT=T[i]["yc"][:, g * P : (g + 1) * P].bitcast(E4M3),
-                        lhsT_scale=T[i]["ys"][:, g * P : (g + 1) * P],
-                        rhs=pw[n][:, g, :].bitcast(E2M1),
-                        rhs_scale=pscale[:, g, n * HALF : (n + 1) * HALF],
-                        start=(g == 0),
-                        stop=(g == KG - 1),
-                    )
+        def mm1(i, n):
+            acc = ps_h.tile([P, HALF], F32, name="h", tag="h")
+            T[i]["h", n] = acc
+            for g in range(KG):
+                nc.tensor.matmul_mx(
+                    out=acc[:],
+                    lhsT=T[i]["yc"][:, g * P : (g + 1) * P].bitcast(E4M3),
+                    lhsT_scale=T[i]["ys"][:, g * P : (g + 1) * P],
+                    rhs=pw[:, g, n * N : (n + 1) * N].bitcast(E2M1),
+                    rhs_scale=pscale[:, g, n * HALF : (n + 1) * HALF],
+                    start=(g == 0),
+                    stop=(g == KG - 1),
+                )
 
-        def sub_u(i):
-            r = work.tile([P, N], F32, name="r")
-            T[i]["r"] = r
-            e = work.tile([P, N], BF16, name="e")
-            T[i]["e"] = e
-            for n in range(2):
-                c = slice(n * HALF, (n + 1) * HALF)
-                nc.vector.tensor_tensor(out=r[:, c], in0=T[i]["h"][n][:], in1=T[i]["u"][:, c], op=SUB)
-                g = slice(n * HALF, min((n + 1) * HALF, gcols(i)))
-                if g.start < g.stop:
-                    nc.gpsimd.tensor_tensor(out=T[i]["e"][:, g], in0=r[:, g], in1=wb[:, g], op=MUL)
+        def sub_u(i, n):
+            if n == 0:
+                r = work.tile([P, N], F32, name="r")
+                e = work.tile([P, N], BF16, name="e")
+                T[i]["r"] = r
+                T[i]["e"] = e
+            c = slice(n * HALF, (n + 1) * HALF)
+            nc.vector.tensor_tensor(out=T[i]["r"][:, c], in0=T[i]["h", n][:], in1=T[i]["u"][:, c], op=SUB)
+
+        def mul_w_g(i, n):
+            g = slice(n * HALF, min((n + 1) * HALF, gcols(i)))
+            if g.start < g.stop:
+                nc.gpsimd.tensor_tensor(out=T[i]["e"][:, g], in0=T[i]["r"][:, g], in1=wb[:, g], op=MUL)
 
         def mul_w_v(i):
-            for c0 in range(gcols(i), N, HALF):
-                c = slice(c0, min(c0 + HALF, N))
+            c = slice(gcols(i), N)
+            if gcols(i) < N:
                 nc.vector.tensor_tensor(out=T[i]["e"][:, c], in0=T[i]["r"][:, c], in1=wb[:, c], op=MUL)
 
         def turn_e(i):
@@ -186,37 +182,35 @@ def tile_lifted_disturbance_observer_s9_kernel(
                 in_=T[i]["eg"][:].rearrange("p g m t -> p (g m t)"),
             )
 
-        def mm2(i):
-            T[i]["d"] = []
-            for n in range(2):
-                acc = ps_d.tile([P, HALF], F32, name="d")
-                T[i]["d"].append(acc)
-                for g in range(NG):
-                    nc.tensor.matmul_mx(
-                        out=acc[:],
-                        lhsT=T[i]["ec"][:, g * P : (g + 1) * P].bitcast(E5M2),
-                        lhsT_scale=T[i]["es"][:, g * P : (g + 1) * P],
-                        rhs=q_codes[:, g, n * HALF : (n + 1) * HALF].bitcast(E4M3),
-                        rhs_scale=q_scale[:, g, n * HALF : (n + 1) * HALF],
-                        start=(g == 0),
-                        stop=(g == NG - 1),
-                    )
+        def mm2(i, n):
+            acc = ps_d.tile([P, HALF], F32, name="d")
+            T[i]["d", n] = acc
+            for g in range(NG):
+                nc.tensor.matmul_mx(
+                    out=acc[:],
+                    lhsT=T[i]["ec"][:, g * P : (g + 1) * P].bitcast(E5M2),
+                    lhsT_scale=T[i]["es"][:, g * P : (g + 1) * P],
+                    rhs=q_codes[:, g, n * HALF : (n + 1) * HALF].bitcast(E4M3),
+                    rhs_scale=q_scale[:, g, n * HALF : (n + 1) * HALF],
+                    start=(g == 0),
+                    stop=(g == NG - 1),
+                )
 
-        def copy_d(i):
-            t = deep.tile([P, N], F32, name="d_sb")
-            T[i]["ds"] = t
-            for n in range(2):
-                nc.scalar.copy(out=t[:, n * HALF : (n + 1) * HALF], in_=T[i]["d"][n][:])
+        def copy_d(i, n):
+            if n == 0:
+                t = deep.tile([P, N], F32, name="d_sb")
+                T[i]["ds"] = t
+            nc.scalar.copy(out=T[i]["ds"][:, n * HALF : (n + 1) * HALF], in_=T[i]["d", n][:])
 
         def store_d(i):
             nc.sync.dma_start(out=out_0[rsl(i), :], in_=T[i]["ds"][:])
 
-        def sub_d(i):
-            t = work.tile([P, N], F32, name="x")
-            T[i]["x"] = t
-            for n in range(2):
-                c = slice(n * HALF, (n + 1) * HALF)
-                nc.vector.tensor_tensor(out=t[:, c], in0=T[i]["c"][:, c], in1=T[i]["d"][n][:], op=SUB)
+        def sub_d(i, n):
+            if n == 0:
+                x = work.tile([P, N], F32, name="x")
+                T[i]["x"] = x
+            c = slice(n * HALF, (n + 1) * HALF)
+            nc.vector.tensor_tensor(out=T[i]["x"][:, c], in0=T[i]["c"][:, c], in1=T[i]["d", n][:], op=SUB)
 
         def cap(i, c):
             nc.vector.tensor_tensor(out=T[i]["x"][:, c], in0=T[i]["x"][:, c], in1=lb[:, c], op=MIN)
@@ -233,7 +227,7 @@ def tile_lifted_disturbance_observer_s9_kernel(
             nc.sync.dma_start(out=out_1[rsl(i), c], in_=T[i]["v"][:, c])
 
         def group_q(n, g, eng):
-            src = q_raw[:, g, n, :, :].rearrange("p j c -> p c j")
+            src = q_raw[:, g, :, n * HALF : (n + 1) * HALF].rearrange("p j c -> p c j")
             if eng == "S":
                 nc.scalar.copy(out=q_grp[:, g, n, :, :], in_=src)
             elif eng == "G":
@@ -248,13 +242,40 @@ def tile_lifted_disturbance_observer_s9_kernel(
                 in_=q_grp[:, g, n, :, :].rearrange("p c j -> p (c j)"),
             )
 
-        ALL = slice(0, N)
+        def bcast(dst_ps, j0):
+            for j in range(8):
+                nc.tensor.transpose(
+                    dst_ps[:, j * P : (j + 1) * P], vcol[:, j0 + j : j0 + j + 1].to_broadcast([P, P]), ident_b[:]
+                )
 
-        def load_p(n):
-            nc.sync.dma_start(
-                out=pw[n][:].bitcast(I32),
-                in_=pinv_words[:, :, n * N : (n + 1) * N].bitcast(I32).rearrange("g p n -> p g n"),
-            )
+        def cap_all(i):
+            w = N if i < TILES - 1 else 256
+            for c0 in range(0, N, w):
+                cap(i, slice(c0, c0 + w))
+
+        def floor_all(i):
+            w = N if i < TILES - 1 else 256
+            for c0 in range(0, N, w):
+                floor_(i, slice(c0, c0 + w))
+                store_v(i, slice(c0, c0 + w))
+
+        def prep():
+            vT = ps_e.tile([P, P], BF16, name="vT", tag="eT")
+            nc.tensor.transpose(vT[:], vec[:], ident_b[:])
+            nc.scalar.copy(out=vcol[:], in_=vT[:, 0:16])
+
+        def spread_w():
+            wB = ps_d.tile([P, N], BF16, name="wB", tag="d")
+            bcast(wB, 0)
+            nc.scalar.copy(out=wb[:], in_=wB[:])
+
+        def spread_l():
+            lB = ps_d.tile([P, N], BF16, name="lB", tag="d")
+            bcast(lB, 8)
+            nc.scalar.copy(out=lb[:], in_=lB[:])
+
+        def load_p(g):
+            nc.sync.dma_start(out=pw[:, g, :].bitcast(I32), in_=pinv_words[g].bitcast(I32))
 
         def load_s():
             for Q in range(4):
@@ -270,18 +291,18 @@ def tile_lifted_disturbance_observer_s9_kernel(
         make_identity(nc, ident_b[:])
         load_y(0)
         load_p(0)
-        load_s()
-        load_u(0)
         load_p(1)
+        load_p(2)
+        load_p(3)
         nc.scalar.dma_start(out=vec[0:8, :], in_=window.rearrange("(a b) -> a b", b=P))
         nc.scalar.dma_start(out=vec[8:16, :], in_=limit.rearrange("(a b) -> a b", b=P))
+        load_s()
+        load_u(0)
         load_y(1)
         load_u(1)
-        load_q(0, 0)
-        load_q(1, 0)
-        load_q(0, 1)
-        load_q(1, 1)
+        load_q(0)
         load_y(2)
+        load_q(1)
         load_u(2)
         load_c(0)
         load_y(3)
@@ -302,80 +323,90 @@ def tile_lifted_disturbance_observer_s9_kernel(
         load_c(6)
         load_c(7)
 
-        turn_y(0)
-        group_y(0)
+
+        def Ty(i):
+            for b in range(2):
+                turn_y(i, b)
+                group_y(i, b)
+
+        def M1(i):
+            for n in range(2):
+                mm1(i, n)
+
+        def U(i):
+            for n in range(2):
+                sub_u(i, n)
+                mul_w_g(i, n)
+
+        def M2(i):
+            for n in range(2):
+                mm2(i, n)
+                copy_d(i, n)
+            store_d(i)
+
+        def X(i):
+            for n in range(2):
+                sub_d(i, n)
+
+        Ty(0)
         quant_y(0)
-        vT = ps_e.tile([P, P], BF16, name="vT", tag="eT")
-        nc.tensor.transpose(vT[:], vec[:], ident_b[:])
-        nc.scalar.copy(out=vcol[:], in_=vT[:, 0:16])
-        wB = ps_d.tile([P, N], BF16, name="wB", tag="d")
-        for j in range(8):
-            nc.tensor.transpose(wB[:, j * P : (j + 1) * P], vcol[:, j : j + 1].to_broadcast([P, P]), ident_b[:])
-        nc.scalar.copy(out=wb[:], in_=wB[:])
-        mm1(0)
-        turn_y(1)
-        group_y(1)
-        sub_u(0)
+        prep()
+        spread_w()
+        spread_l()
+        M1(0)
+        Ty(1)
+        U(0)
         mul_w_v(0)
         turn_e(0)
         group_e(0)
         quant_y(1)
-        mm1(1)
+        M1(1)
+        group_q(0, 0, "S")
+        Ty(2)
+        group_q(1, 0, "V")
         quant_e(0)
-        for n, g in ((0, 0), (0, 1), (1, 0), (1, 1)):
-            group_q(n, g, QE[2 * n + g])
-            quant_q(n, g)
-            if n == 0 and g == 1:
-                turn_y(2)
-                group_y(2)
-                sub_u(1)
-                mul_w_v(1)
-        mm2(0)
-        turn_e(1)
-        group_e(1)
+        U(1)
+        quant_q(1, 0)
+        mul_w_v(1)
+        quant_q(0, 0)
         quant_y(2)
-        mm1(2)
-        copy_d(0)
-        store_d(0)
-        lB = ps_d.tile([P, N], BF16, name="lB", tag="d")
-        for j in range(8):
-            nc.tensor.transpose(lB[:, j * P : (j + 1) * P], vcol[:, 8 + j : 9 + j].to_broadcast([P, P]), ident_b[:])
-        nc.scalar.copy(out=lb[:], in_=lB[:])
-        turn_y(3)
-        group_y(3)
+        group_q(0, 1, "V")
+        group_q(1, 1, "S")
+        turn_e(1)
+        M1(2)
+        quant_q(0, 1)
+        quant_q(1, 1)
+        M2(0)
+        Ty(3)
+        group_e(1)
+        X(0)
         quant_e(1)
-        EARLY = False
+        cap_all(0)
+        quant_y(3)
+        floor_all(0)
+        Ty(4)
         for s in range(2, TILES + 2):
             i = s - 2
             if s < TILES:
-                sub_u(s)
-            if s + 1 < TILES:
-                quant_y(s + 1)
-                mm1(s + 1)
-            if s - 1 < TILES:
-                mm2(s - 1)
-            if i > 0 or not EARLY:
-                sub_d(i)
+                U(s)
+            if i > 0:
+                X(i)
+            if 1 < s - 1 < TILES:
+                quant_e(s - 1)
             if s < TILES:
                 mul_w_v(s)
+            if s + 1 < TILES:
+                M1(s + 1)
             if s - 1 < TILES:
-                copy_d(s - 1)
-                store_d(s - 1)
+                M2(s - 1)
             if s < TILES:
                 turn_e(s)
                 group_e(s)
-                quant_e(s)
+            if s + 3 < TILES:
+                Ty(s + 3)
+            if i > 0:
+                cap_all(i)
             if s + 2 < TILES:
-                turn_y(s + 2)
-                group_y(s + 2)
-            if i > 0 or not EARLY:
-                if i < TILES - 1:
-                    cap(i, ALL)
-                    floor_(i, ALL)
-                    store_v(i, ALL)
-                else:
-                    for c0 in range(0, N, 256):
-                        cap(i, slice(c0, c0 + 256))
-                    for c0 in range(0, N, 256):
-                        floor_(i, slice(c0, c0 + 256))
-                        store_v(i, slice(c0, c0 + 256))
+                quant_y(s + 2)
+            if i > 0:
+                floor_all(i)

@@ -28,8 +28,6 @@ NG = N // 512
 TILES = M // P
 HALF = 512
 QE = ""
-GCOLS = 512
-GFILL = 512
 
 
 def tile_lifted_disturbance_observer_s9_kernel(
@@ -44,26 +42,27 @@ def tile_lifted_disturbance_observer_s9_kernel(
         ps_y = ctx.enter_context(tc.psum_pool(name="ps_y", bufs=2))
         ps_e = ctx.enter_context(tc.psum_pool(name="ps_e", bufs=1))
         ps_h = ctx.enter_context(tc.psum_pool(name="ps_h", bufs=2))
-        ps_d = ctx.enter_context(tc.psum_pool(name="ps_d", bufs=3))
+        ps_d = ctx.enter_context(tc.psum_pool(name="ps_d", bufs=2))
+        ps_r = ctx.enter_context(tc.psum_pool(name="ps_r", bufs=1))
         ctx.enter_context(tc.manual_schedule())
 
         ident = keep.tile([P, P], F32, name="ident")
         ident_b = keep.tile([P, P], BF16, name="ident_b")
         vec = keep.tile([P, P], BF16, name="vec")
         vcol = keep.tile([P, 16], BF16, name="vcol")
-        wb = keep.tile([P, N], BF16, name="wb")
+        wb = keep.tile([P, HALF], BF16, name="wb")
+        wcol_b = keep.tile([P, PACK], BF16, name="wcol_b")
+        wcol = keep.tile([P, PACK], F32, name="wcol")
+        warm = keep.tile([P, 1], F32, name="warm")
         lb = keep.tile([P, N], BF16, name="lb")
         pw = keep.tile([P, KG, 2 * N], U8, name="pw", align_bytes=64)
         pscale = keep.tile([P, KG, N], U8, name="pscale", align_bytes=64)
-        q_raw = keep.tile([P, NG, PACK, N], BF16, name="q_raw")
+        q_raw = keep.tile([P, NG, 2, PACK, HALF], BF16, name="q_raw")
         q_grp = keep.tile([P, NG, 2, HALF, PACK], BF16, name="q_grp", align_bytes=64)
         q_codes = keep.tile([P, NG, N], U32, name="q_codes", align_bytes=64)
         q_scale = keep.tile([P, NG, N], U8, name="q_scale", align_bytes=64)
 
         T = [dict() for i in range(TILES)]
-
-        def gcols(i):
-            return GFILL if i < 2 else GCOLS
 
         def rsl(i):
             return slice(i * P, (i + 1) * P)
@@ -85,10 +84,11 @@ def tile_lifted_disturbance_observer_s9_kernel(
             T[i]["c"] = t
             nc.sync.dma_start(out=t[:], in_=command[rsl(i), :])
 
-        def load_q(g):
+        def load_q(g, n):
+            c = slice(n * HALF, (n + 1) * HALF)
             nc.sync.dma_start(
-                out=q_raw[:, g, :, :],
-                in_=qfilter[g * 512 : (g + 1) * 512, :].rearrange("(p j) n -> p j n", j=PACK),
+                out=q_raw[:, g, n, :, :],
+                in_=qfilter[g * 512 : (g + 1) * 512, c].rearrange("(p j) n -> p j n", j=PACK),
             )
 
         def turn_y(i, b):
@@ -136,40 +136,66 @@ def tile_lifted_disturbance_observer_s9_kernel(
                     stop=(g == KG - 1),
                 )
 
-        def sub_u(i, n):
-            if n == 0:
-                r = work.tile([P, N], F32, name="r")
-                e = work.tile([P, N], BF16, name="e")
-                T[i]["r"] = r
-                T[i]["e"] = e
-            c = slice(n * HALF, (n + 1) * HALF)
-            nc.vector.tensor_tensor(out=T[i]["r"][:, c], in0=T[i]["h", n][:], in1=T[i]["u"][:, c], op=SUB)
+        def sub_u0(i):
+            r = work.tile([P, 2, P, 2], F32, name="r0")
+            T[i]["r0"] = r
+            nc.vector.tensor_tensor(
+                out=r[:],
+                in0=T[i]["h", 0][:].rearrange("p (w h e) -> p h w e", h=2, e=2),
+                in1=T[i]["u"][:, 0:HALF].rearrange("p (w h e) -> p h w e", h=2, e=2),
+                op=SUB,
+            )
 
-        def mul_w_g(i, n):
-            g = slice(n * HALF, min((n + 1) * HALF, gcols(i)))
-            if g.start < g.stop:
-                nc.gpsimd.tensor_tensor(out=T[i]["e"][:, g], in0=T[i]["r"][:, g], in1=wb[:, g], op=MUL)
+        def sub_u1(i):
+            r = work.tile([P, PACK, P], F32, name="r1")
+            T[i]["r1"] = r
+            nc.vector.tensor_tensor(
+                out=r[:],
+                in0=T[i]["h", 1][:].rearrange("p (w t) -> p t w", t=PACK),
+                in1=T[i]["u"][:, HALF:N].rearrange("p (w t) -> p t w", t=PACK),
+                op=SUB,
+            )
 
-        def mul_w_v(i):
-            c = slice(gcols(i), N)
-            if gcols(i) < N:
-                nc.vector.tensor_tensor(out=T[i]["e"][:, c], in0=T[i]["r"][:, c], in1=wb[:, c], op=MUL)
+        def mul_w(i, eng="V"):
+            e = work.tile([P, HALF], BF16, name="e")
+            T[i]["e"] = e
+            (nc.vector if eng == "V" else nc.gpsimd).tensor_tensor(
+                out=e[:], in0=T[i]["r0"][:].rearrange("p h w e -> p (h w e)"), in1=wb[:], op=MUL
+            )
 
         def turn_e(i):
             words = T[i]["e"][:].bitcast(F32)
-            bank = ps_e.tile([P, NG, 2, P], F32, name="eT")
+            bank = ps_e.tile([P, 2, P], F32, name="eT", tag="eT")
             T[i]["eT"] = bank
-            for g in range(NG):
-                for h in range(2):
-                    nc.tensor.transpose(bank[:, g, h, :], words[:, 256 * g + h : 256 * (g + 1) : 2], ident[:])
+            for h in range(2):
+                nc.tensor.transpose(bank[:, h, :], words[:, h * P : (h + 1) * P], ident[:])
+
+        def turn_r(i):
+            bank = ps_r.tile([P, PACK, P], F32, name="rT")
+            T[i]["rT"] = bank
+            for t in range(PACK):
+                nc.tensor.transpose(bank[:, t, :], T[i]["r1"][:, t, :], ident[:])
 
         def group_e(i):
             grp = work.tile([P, NG, P, PACK], BF16, name="e_grp", align_bytes=64)
             T[i]["eg"] = grp
-            wv = grp[:].rearrange("p g m t -> p (g m t)").bitcast(F32)
+            wv = grp[:, 0, :, :].rearrange("p m t -> p (m t)").bitcast(F32)
             nc.scalar.copy(
-                out=wv.rearrange("p (g m h) -> p g m h", g=NG, h=2),
-                in_=T[i]["eT"][:].rearrange("p g h m -> p g m h"),
+                out=wv.rearrange("p (m h) -> p m h", h=2),
+                in_=T[i]["eT"][:].rearrange("p h m -> p m h"),
+            )
+
+        def scale_r(i):
+            es = work.tile([P, PACK, P], BF16, name="es")
+            T[i]["es_raw"] = es
+            for t in range(PACK):
+                nc.scalar.activation(
+                    out=es[:, t, :], in_=T[i]["rT"][:, t, :], func=COPY, scale=wcol[:, t : t + 1]
+                )
+
+        def group_r(i):
+            nc.scalar.copy(
+                out=T[i]["eg"][:, 1, :, :], in_=T[i]["es_raw"][:].rearrange("p t m -> p m t")
             )
 
         def quant_e(i):
@@ -227,7 +253,7 @@ def tile_lifted_disturbance_observer_s9_kernel(
             nc.sync.dma_start(out=out_1[rsl(i), c], in_=T[i]["v"][:, c])
 
         def group_q(n, g, eng):
-            src = q_raw[:, g, :, n * HALF : (n + 1) * HALF].rearrange("p j c -> p c j")
+            src = q_raw[:, g, n, :, :].rearrange("p j c -> p c j")
             if eng == "S":
                 nc.scalar.copy(out=q_grp[:, g, n, :, :], in_=src)
             elif eng == "G":
@@ -242,8 +268,8 @@ def tile_lifted_disturbance_observer_s9_kernel(
                 in_=q_grp[:, g, n, :, :].rearrange("p c j -> p (c j)"),
             )
 
-        def bcast(dst_ps, j0):
-            for j in range(8):
+        def bcast(dst_ps, j0, count):
+            for j in range(count):
                 nc.tensor.transpose(
                     dst_ps[:, j * P : (j + 1) * P], vcol[:, j0 + j : j0 + j + 1].to_broadcast([P, P]), ident_b[:]
                 )
@@ -265,13 +291,17 @@ def tile_lifted_disturbance_observer_s9_kernel(
             nc.scalar.copy(out=vcol[:], in_=vT[:, 0:16])
 
         def spread_w():
-            wB = ps_d.tile([P, N], BF16, name="wB", tag="d")
-            bcast(wB, 0)
-            nc.scalar.copy(out=wb[:], in_=wB[:])
+            wB = ps_d.tile([P, HALF], BF16, name="wB", tag="d")
+            bcast(wB, 0, 4)
+            nc.scalar.copy(
+                out=wb[:].rearrange("p (h w e) -> p h w e", h=2, e=2),
+                in_=wB[:].rearrange("p (w h e) -> p h w e", h=2, e=2),
+            )
+            nc.scalar.copy(out=wcol[:], in_=wcol_b[:])
 
         def spread_l():
             lB = ps_d.tile([P, N], BF16, name="lB", tag="d")
-            bcast(lB, 8)
+            bcast(lB, 8, 8)
             nc.scalar.copy(out=lb[:], in_=lB[:])
 
         def load_p(g):
@@ -285,26 +315,31 @@ def tile_lifted_disturbance_observer_s9_kernel(
                 )
 
         ps32 = pscale[:].rearrange("p g n -> p (g n)").bitcast(I32)
-        nc.vector.memset(vec[:], 0.0)
+        nc.vector.memset(warm[:], 0.0)
         nc.vector.memset(ps32, 0)
+        nc.vector.memset(vec[:], 0.0)
+        nc.scalar.copy(out=warm[:], in_=warm[:])
         make_identity(nc, ident[:])
         make_identity(nc, ident_b[:])
         load_y(0)
+        load_s()
         load_p(0)
         load_p(1)
         load_p(2)
         load_p(3)
         nc.scalar.dma_start(out=vec[0:8, :], in_=window.rearrange("(a b) -> a b", b=P))
         nc.scalar.dma_start(out=vec[8:16, :], in_=limit.rearrange("(a b) -> a b", b=P))
-        load_s()
+        nc.scalar.dma_start(out=wcol_b[:], in_=window[HALF:N].rearrange("(p t) -> p t", t=PACK))
         load_u(0)
         load_y(1)
         load_u(1)
-        load_q(0)
-        load_y(2)
-        load_q(1)
-        load_u(2)
+        load_q(0, 0)
+        load_q(1, 0)
+        load_q(0, 1)
+        load_q(1, 1)
         load_c(0)
+        load_y(2)
+        load_u(2)
         load_y(3)
         load_u(3)
         load_c(1)
@@ -323,90 +358,220 @@ def tile_lifted_disturbance_observer_s9_kernel(
         load_c(6)
         load_c(7)
 
+        def Ty(i, b):
+            turn_y(i, b)
 
-        def Ty(i):
-            for b in range(2):
-                turn_y(i, b)
-                group_y(i, b)
+        def Gy(i, b):
+            group_y(i, b)
 
-        def M1(i):
-            for n in range(2):
-                mm1(i, n)
-
-        def U(i):
-            for n in range(2):
-                sub_u(i, n)
-                mul_w_g(i, n)
-
-        def M2(i):
-            for n in range(2):
-                mm2(i, n)
-                copy_d(i, n)
-            store_d(i)
-
-        def X(i):
-            for n in range(2):
-                sub_d(i, n)
-
-        Ty(0)
-        quant_y(0)
+        Ty(0, 0)
+        Gy(0, 0)
+        Ty(0, 1)
+        Gy(0, 1)
         prep()
         spread_w()
         spread_l()
-        M1(0)
-        Ty(1)
-        U(0)
-        mul_w_v(0)
+        quant_y(0)
+        mm1(0, 0)
+        mm1(0, 1)
+        sub_u0(0)
+        mul_w(0)
+        Ty(1, 0)
+        sub_u1(0)
+        turn_r(0)
+        Gy(1, 0)
+        scale_r(0)
         turn_e(0)
+        group_q(0, 0, "V")
         group_e(0)
-        quant_y(1)
-        M1(1)
-        group_q(0, 0, "S")
-        Ty(2)
-        group_q(1, 0, "V")
+        group_r(0)
         quant_e(0)
-        U(1)
-        quant_q(1, 0)
-        mul_w_v(1)
+        Ty(1, 1)
+        group_q(0, 1, "S")
+        Gy(1, 1)
         quant_q(0, 0)
-        quant_y(2)
-        group_q(0, 1, "V")
-        group_q(1, 1, "S")
-        turn_e(1)
-        M1(2)
+        group_q(1, 0, "V")
         quant_q(0, 1)
-        quant_q(1, 1)
-        M2(0)
-        Ty(3)
+        group_q(1, 1, "S")
+        quant_y(1)
+        mm2(0, 0)
+        mm1(1, 0)
+        quant_q(1, 0)
+        mm1(1, 1)
+        sub_u0(1)
+        Ty(2, 0)
+        mul_w(1)
+        Gy(2, 0)
+        turn_e(1)
         group_e(1)
-        X(0)
-        quant_e(1)
+        sub_u1(1)
+        Ty(2, 1)
+        Gy(2, 1)
+        quant_q(1, 1)
+        mm2(0, 1)
+        Ty(3, 0)
+        Ty(3, 1)
+        Gy(3, 0)
+        Gy(3, 1)
+        sub_d(0, 0)
+        sub_d(0, 1)
+        turn_r(1)
+        scale_r(1)
+        copy_d(0, 0)
+        quant_y(2)
+        mm1(2, 0)
         cap_all(0)
-        quant_y(3)
         floor_all(0)
-        Ty(4)
-        for s in range(2, TILES + 2):
-            i = s - 2
-            if s < TILES:
-                U(s)
-            if i > 0:
-                X(i)
-            if 1 < s - 1 < TILES:
-                quant_e(s - 1)
-            if s < TILES:
-                mul_w_v(s)
-            if s + 1 < TILES:
-                M1(s + 1)
-            if s - 1 < TILES:
-                M2(s - 1)
-            if s < TILES:
-                turn_e(s)
-                group_e(s)
-            if s + 3 < TILES:
-                Ty(s + 3)
-            if i > 0:
-                cap_all(i)
-            if s + 2 < TILES:
-                quant_y(s + 2)
-            if i > 0:
-                floor_all(i)
+        Ty(4, 0)
+        Ty(4, 1)
+        quant_y(3)
+        mm1(2, 1)
+        sub_u0(2)
+        group_r(1)
+        quant_e(1)
+        mm1(3, 0)
+        Gy(4, 0)
+        Gy(4, 1)
+        quant_y(4)
+        copy_d(0, 1)
+        store_d(0)
+        mm2(1, 0)
+        copy_d(1, 0)
+        mm2(1, 1)
+        sub_u1(2)
+        sub_u0(3)
+        mm1(3, 1)
+        mul_w(2)
+        mul_w(3)
+        copy_d(1, 1)
+        sub_d(1, 0)
+        sub_d(1, 1)
+        sub_u1(3)
+        cap_all(1)
+        turn_r(2)
+        scale_r(2)
+        turn_e(2)
+        group_e(2)
+        group_r(2)
+        quant_e(2)
+        floor_all(1)
+        Ty(5, 0)
+        Ty(5, 1)
+        Gy(5, 0)
+        mm1(4, 0)
+        sub_u0(4)
+        Gy(5, 1)
+        mm2(2, 0)
+        copy_d(2, 0)
+        sub_d(2, 0)
+        mm2(2, 1)
+        copy_d(2, 1)
+        turn_e(3)
+        turn_r(3)
+        sub_d(2, 1)
+        quant_y(5)
+        mm1(4, 1)
+        sub_u1(4)
+        group_e(3)
+        scale_r(3)
+        cap_all(2)
+        group_r(3)
+        quant_e(3)
+        Ty(6, 0)
+        Ty(6, 1)
+        mm1(5, 0)
+        mm2(3, 0)
+        mul_w(4)
+        turn_r(4)
+        mm2(3, 1)
+        floor_all(2)
+        Gy(6, 0)
+        Gy(6, 1)
+        turn_e(4)
+        sub_u0(5)
+        copy_d(3, 0)
+        sub_d(3, 0)
+        copy_d(3, 1)
+        sub_d(3, 1)
+        mm1(5, 1)
+        group_e(4)
+        quant_y(6)
+        sub_u1(5)
+        scale_r(4)
+        group_r(4)
+        quant_e(4)
+        store_d(1)
+        Ty(7, 0)
+        Gy(7, 0)
+        Ty(7, 1)
+        Gy(7, 1)
+        store_d(2)
+        store_d(3)
+        mul_w(5)
+        mm1(6, 0)
+        mm1(6, 1)
+        mm2(4, 0)
+        mm2(4, 1)
+        copy_d(4, 0)
+        copy_d(4, 1)
+        store_d(4)
+        turn_e(5)
+        turn_r(5)
+        group_e(5)
+        scale_r(5)
+        group_r(5)
+        cap_all(3)
+        quant_y(7)
+        floor_all(3)
+        sub_u0(6)
+        sub_u1(6)
+        sub_d(4, 0)
+        sub_d(4, 1)
+        quant_e(5)
+        mul_w(6)
+        mm1(7, 0)
+        mm1(7, 1)
+        mm2(5, 0)
+        mm2(5, 1)
+        copy_d(5, 0)
+        copy_d(5, 1)
+        store_d(5)
+        turn_e(6)
+        turn_r(6)
+        group_e(6)
+        scale_r(6)
+        group_r(6)
+        cap_all(4)
+        floor_all(4)
+        sub_u0(7)
+        sub_u1(7)
+        sub_d(5, 0)
+        sub_d(5, 1)
+        quant_e(6)
+        mul_w(7)
+        mm2(6, 0)
+        mm2(6, 1)
+        copy_d(6, 0)
+        copy_d(6, 1)
+        store_d(6)
+        turn_e(7)
+        turn_r(7)
+        group_e(7)
+        scale_r(7)
+        group_r(7)
+        cap_all(5)
+        floor_all(5)
+        sub_d(6, 0)
+        sub_d(6, 1)
+        quant_e(7)
+        mm2(7, 0)
+        mm2(7, 1)
+        copy_d(7, 0)
+        copy_d(7, 1)
+        store_d(7)
+        cap_all(6)
+        floor_all(6)
+        sub_d(7, 0)
+        sub_d(7, 1)
+        cap_all(7)
+        floor_all(7)

@@ -40,24 +40,23 @@ def tile_lifted_disturbance_observer_s9_kernel(
         work = ctx.enter_context(tc.tile_pool(name="work", bufs=3))
         deep = ctx.enter_context(tc.tile_pool(name="deep", bufs=3))
         ps_y = ctx.enter_context(tc.psum_pool(name="ps_y", bufs=2))
-        ps_e = ctx.enter_context(tc.psum_pool(name="ps_e", bufs=1))
         ps_h = ctx.enter_context(tc.psum_pool(name="ps_h", bufs=2))
         ps_d = ctx.enter_context(tc.psum_pool(name="ps_d", bufs=2))
-        ps_r = ctx.enter_context(tc.psum_pool(name="ps_r", bufs=1))
+        ps_r = ctx.enter_context(tc.psum_pool(name="ps_r", bufs=2))
         ctx.enter_context(tc.manual_schedule())
 
         ident = keep.tile([P, P], F32, name="ident")
         ident_b = keep.tile([P, P], BF16, name="ident_b")
         vec = keep.tile([P, P], BF16, name="vec")
-        vcol = keep.tile([P, 16], BF16, name="vcol")
-        wb = keep.tile([P, HALF], BF16, name="wb")
-        wcol_b = keep.tile([P, PACK], BF16, name="wcol_b")
-        wcol = keep.tile([P, PACK], F32, name="wcol")
+        vcol = keep.tile([P, 8], BF16, name="vcol")
+        wcol_b = keep.tile([P, NG, PACK], BF16, name="wcol_b")
+        wcol = keep.tile([P, NG, PACK], F32, name="wcol")
         warm = keep.tile([P, 1], F32, name="warm")
         lb = keep.tile([P, N], BF16, name="lb")
+        nlb = keep.tile([P, N], BF16, name="nlb")
         pw = keep.tile([P, KG, 2 * N], U8, name="pw", align_bytes=64)
         pscale = keep.tile([P, KG, N], U8, name="pscale", align_bytes=64)
-        q_raw = keep.tile([P, NG, 2, PACK, HALF], BF16, name="q_raw")
+        q_raw = keep.tile([P, NG, PACK, N], BF16, name="q_raw")
         q_grp = keep.tile([P, NG, 2, HALF, PACK], BF16, name="q_grp", align_bytes=64)
         q_codes = keep.tile([P, NG, N], U32, name="q_codes", align_bytes=64)
         q_scale = keep.tile([P, NG, N], U8, name="q_scale", align_bytes=64)
@@ -84,11 +83,10 @@ def tile_lifted_disturbance_observer_s9_kernel(
             T[i]["c"] = t
             nc.sync.dma_start(out=t[:], in_=command[rsl(i), :])
 
-        def load_q(g, n):
-            c = slice(n * HALF, (n + 1) * HALF)
+        def load_q(g):
             nc.sync.dma_start(
-                out=q_raw[:, g, n, :, :],
-                in_=qfilter[g * 512 : (g + 1) * 512, c].rearrange("(p j) n -> p j n", j=PACK),
+                out=q_raw[:, g, :, :],
+                in_=qfilter[g * 512 : (g + 1) * 512, :].rearrange("(p j) n -> p j n", j=PACK),
             )
 
         def turn_y(i, b):
@@ -136,66 +134,40 @@ def tile_lifted_disturbance_observer_s9_kernel(
                     stop=(g == KG - 1),
                 )
 
-        def sub_u0(i):
-            r = work.tile([P, 2, P, 2], F32, name="r0")
-            T[i]["r0"] = r
+        def sub_u(i, n):
+            if n == 0:
+                r = work.tile([P, NG, PACK, P], F32, name="r")
+                T[i]["r"] = r
+            c = slice(n * HALF, (n + 1) * HALF)
             nc.vector.tensor_tensor(
-                out=r[:],
-                in0=T[i]["h", 0][:].rearrange("p (w h e) -> p h w e", h=2, e=2),
-                in1=T[i]["u"][:, 0:HALF].rearrange("p (w h e) -> p h w e", h=2, e=2),
+                out=T[i]["r"][:, n, :, :],
+                in0=T[i]["h", n][:].rearrange("p (w t) -> p t w", t=PACK),
+                in1=T[i]["u"][:, c].rearrange("p (w t) -> p t w", t=PACK),
                 op=SUB,
             )
 
-        def sub_u1(i):
-            r = work.tile([P, PACK, P], F32, name="r1")
-            T[i]["r1"] = r
-            nc.vector.tensor_tensor(
-                out=r[:],
-                in0=T[i]["h", 1][:].rearrange("p (w t) -> p t w", t=PACK),
-                in1=T[i]["u"][:, HALF:N].rearrange("p (w t) -> p t w", t=PACK),
-                op=SUB,
-            )
-
-        def mul_w(i, eng="V"):
-            e = work.tile([P, HALF], BF16, name="e")
-            T[i]["e"] = e
-            (nc.vector if eng == "V" else nc.gpsimd).tensor_tensor(
-                out=e[:], in0=T[i]["r0"][:].rearrange("p h w e -> p (h w e)"), in1=wb[:], op=MUL
-            )
-
-        def turn_e(i):
-            words = T[i]["e"][:].bitcast(F32)
-            bank = ps_e.tile([P, 2, P], F32, name="eT", tag="eT")
-            T[i]["eT"] = bank
-            for h in range(2):
-                nc.tensor.transpose(bank[:, h, :], words[:, h * P : (h + 1) * P], ident[:])
-
-        def turn_r(i):
-            bank = ps_r.tile([P, PACK, P], F32, name="rT")
-            T[i]["rT"] = bank
+        def turn_r(i, n):
+            bank = ps_r.tile([P, PACK, P], F32, name="rT", tag="rT")
+            T[i]["rT", n] = bank
             for t in range(PACK):
-                nc.tensor.transpose(bank[:, t, :], T[i]["r1"][:, t, :], ident[:])
+                nc.tensor.transpose(bank[:, t, :], T[i]["r"][:, n, t, :], ident[:])
 
-        def group_e(i):
-            grp = work.tile([P, NG, P, PACK], BF16, name="e_grp", align_bytes=64)
-            T[i]["eg"] = grp
-            wv = grp[:, 0, :, :].rearrange("p m t -> p (m t)").bitcast(F32)
-            nc.scalar.copy(
-                out=wv.rearrange("p (m h) -> p m h", h=2),
-                in_=T[i]["eT"][:].rearrange("p h m -> p m h"),
-            )
-
-        def scale_r(i):
-            es = work.tile([P, PACK, P], BF16, name="es")
-            T[i]["es_raw"] = es
+        def scale_r(i, n):
+            if n == 0:
+                e = work.tile([P, NG, PACK, P], BF16, name="e")
+                T[i]["e"] = e
             for t in range(PACK):
                 nc.scalar.activation(
-                    out=es[:, t, :], in_=T[i]["rT"][:, t, :], func=COPY, scale=wcol[:, t : t + 1]
+                    out=T[i]["e"][:, n, t, :], in_=T[i]["rT", n][:, t, :], func=COPY, scale=wcol[:, n, t : t + 1]
                 )
 
-        def group_r(i):
+        def group_e(i, n):
+            if n == 0:
+                grp = work.tile([P, NG, P, PACK], BF16, name="e_grp", align_bytes=64)
+                T[i]["eg"] = grp
             nc.scalar.copy(
-                out=T[i]["eg"][:, 1, :, :], in_=T[i]["es_raw"][:].rearrange("p t m -> p m t")
+                out=T[i]["eg"][:, n, :, :].rearrange("p (c k) t -> p c t k", k=4),
+                in_=T[i]["e"][:, n, :, :].rearrange("p t (c k) -> p c t k", k=4),
             )
 
         def quant_e(i):
@@ -245,21 +217,20 @@ def tile_lifted_disturbance_observer_s9_kernel(
             if "v" not in T[i]:
                 t = deep.tile([P, N], F32, name="v")
                 T[i]["v"] = t
-            nc.vector.scalar_tensor_tensor(
-                out=T[i]["v"][:, c], in0=lb[:, c], scalar=-1.0, in1=T[i]["x"][:, c], op0=MUL, op1=MAX
-            )
+            nc.vector.tensor_tensor(out=T[i]["v"][:, c], in0=T[i]["x"][:, c], in1=nlb[:, c], op=MAX)
 
         def store_v(i, c):
             nc.sync.dma_start(out=out_1[rsl(i), c], in_=T[i]["v"][:, c])
 
         def group_q(n, g, eng):
-            src = q_raw[:, g, n, :, :].rearrange("p j c -> p c j")
+            src = q_raw[:, g, :, n * HALF : (n + 1) * HALF].rearrange("p j (c k) -> p c j k", k=4)
+            dst = q_grp[:, g, n, :, :].rearrange("p (c k) j -> p c j k", k=4)
             if eng == "S":
-                nc.scalar.copy(out=q_grp[:, g, n, :, :], in_=src)
+                nc.scalar.copy(out=dst, in_=src)
             elif eng == "G":
-                nc.gpsimd.tensor_scalar(out=q_grp[:, g, n, :, :], in0=src, scalar1=1.0, scalar2=0.0, op0=MUL, op1=ADD)
+                nc.gpsimd.tensor_scalar(out=dst, in0=src, scalar1=1.0, scalar2=0.0, op0=MUL, op1=ADD)
             else:
-                nc.vector.tensor_copy(out=q_grp[:, g, n, :, :], in_=src)
+                nc.vector.tensor_copy(out=dst, in_=src)
 
         def quant_q(n, g):
             c = slice(n * HALF, (n + 1) * HALF)
@@ -286,23 +257,16 @@ def tile_lifted_disturbance_observer_s9_kernel(
                 store_v(i, slice(c0, c0 + w))
 
         def prep():
-            vT = ps_e.tile([P, P], BF16, name="vT", tag="eT")
+            nc.vector.tensor_copy(out=wcol[:], in_=wcol_b[:])
+            vT = ps_r.tile([P, P], BF16, name="vT", tag="rT")
             nc.tensor.transpose(vT[:], vec[:], ident_b[:])
-            nc.scalar.copy(out=vcol[:], in_=vT[:, 0:16])
-
-        def spread_w():
-            wB = ps_d.tile([P, HALF], BF16, name="wB", tag="d")
-            bcast(wB, 0, 4)
-            nc.scalar.copy(
-                out=wb[:].rearrange("p (h w e) -> p h w e", h=2, e=2),
-                in_=wB[:].rearrange("p (w h e) -> p h w e", h=2, e=2),
-            )
-            nc.scalar.copy(out=wcol[:], in_=wcol_b[:])
+            nc.scalar.copy(out=vcol[:], in_=vT[:, 0:8])
 
         def spread_l():
             lB = ps_d.tile([P, N], BF16, name="lB", tag="d")
-            bcast(lB, 8, 8)
+            bcast(lB, 0, 8)
             nc.scalar.copy(out=lb[:], in_=lB[:])
+            nc.gpsimd.tensor_scalar(out=nlb[:], in0=lb[:], scalar1=-1.0, scalar2=0.0, op0=MUL, op1=ADD)
 
         def load_p(g):
             nc.sync.dma_start(out=pw[:, g, :].bitcast(I32), in_=pinv_words[g].bitcast(I32))
@@ -327,19 +291,16 @@ def tile_lifted_disturbance_observer_s9_kernel(
         load_p(1)
         load_p(2)
         load_p(3)
-        nc.scalar.dma_start(out=vec[0:8, :], in_=window.rearrange("(a b) -> a b", b=P))
-        nc.scalar.dma_start(out=vec[8:16, :], in_=limit.rearrange("(a b) -> a b", b=P))
-        nc.scalar.dma_start(out=wcol_b[:], in_=window[HALF:N].rearrange("(p t) -> p t", t=PACK))
+        nc.scalar.dma_start(out=vec[0:8, :], in_=limit.rearrange("(a b) -> a b", b=P))
+        nc.scalar.dma_start(out=wcol_b[:], in_=window.rearrange("(g p t) -> p g t", p=P, t=PACK))
         load_u(0)
         load_y(1)
         load_u(1)
-        load_q(0, 0)
-        load_q(1, 0)
-        load_q(0, 1)
-        load_q(1, 1)
-        load_c(0)
+        load_q(0)
         load_y(2)
+        load_q(1)
         load_u(2)
+        load_c(0)
         load_y(3)
         load_u(3)
         load_c(1)
@@ -368,210 +329,209 @@ def tile_lifted_disturbance_observer_s9_kernel(
         Gy(0, 0)
         Ty(0, 1)
         Gy(0, 1)
-        prep()
-        spread_w()
-        spread_l()
         quant_y(0)
+        prep()
+        spread_l()
         mm1(0, 0)
-        mm1(0, 1)
-        sub_u0(0)
-        mul_w(0)
+        sub_u(0, 0)
         Ty(1, 0)
-        sub_u1(0)
-        turn_r(0)
-        Gy(1, 0)
-        scale_r(0)
-        turn_e(0)
-        group_q(0, 0, "V")
-        group_e(0)
-        group_r(0)
-        quant_e(0)
         Ty(1, 1)
-        group_q(0, 1, "S")
+        Gy(1, 0)
+        group_q(1, 0, "G")
+        turn_r(0, 0)
         Gy(1, 1)
-        quant_q(0, 0)
-        group_q(1, 0, "V")
-        quant_q(0, 1)
-        group_q(1, 1, "S")
         quant_y(1)
-        mm2(0, 0)
+        mm1(0, 1)
         mm1(1, 0)
-        quant_q(1, 0)
-        mm1(1, 1)
-        sub_u0(1)
         Ty(2, 0)
-        mul_w(1)
-        Gy(2, 0)
-        turn_e(1)
-        group_e(1)
-        sub_u1(1)
+        group_q(0, 0, "S")
         Ty(2, 1)
+        sub_u(0, 1)
+        sub_u(1, 0)
+        scale_r(0, 0)
+        Gy(2, 0)
+        turn_r(0, 1)
+        scale_r(0, 1)
+        quant_q(0, 0)
+        mm1(1, 1)
+        group_q(1, 1, "V")
+        sub_u(1, 1)
         Gy(2, 1)
-        quant_q(1, 1)
-        mm2(0, 1)
+        turn_r(1, 0)
+        turn_r(1, 1)
+        group_e(0, 0)
+        group_e(0, 1)
         Ty(3, 0)
+        quant_y(2)
+        group_q(0, 1, "V")
+        scale_r(1, 0)
+        quant_e(0)
+        quant_q(1, 0)
+        mm1(2, 0)
+        quant_q(0, 1)
         Ty(3, 1)
         Gy(3, 0)
-        Gy(3, 1)
-        sub_d(0, 0)
-        sub_d(0, 1)
-        turn_r(1)
-        scale_r(1)
-        copy_d(0, 0)
-        quant_y(2)
-        mm1(2, 0)
-        cap_all(0)
-        floor_all(0)
         Ty(4, 0)
-        Ty(4, 1)
+        quant_q(1, 1)
+        sub_u(2, 0)
+        mm2(0, 0)
+        sub_d(0, 0)
+        mm2(0, 1)
+        sub_d(0, 1)
+        scale_r(1, 1)
+        Gy(3, 1)
         quant_y(3)
         mm1(2, 1)
-        sub_u0(2)
-        group_r(1)
+        group_e(1, 0)
+        group_e(1, 1)
+        copy_d(0, 0)
+        copy_d(0, 1)
+        Gy(4, 0)
+        sub_u(2, 1)
+        turn_r(2, 0)
+        Ty(4, 1)
+        turn_r(2, 1)
+        Gy(4, 1)
+        store_d(0)
         quant_e(1)
         mm1(3, 0)
-        Gy(4, 0)
-        Gy(4, 1)
-        quant_y(4)
-        copy_d(0, 1)
-        store_d(0)
+        scale_r(2, 0)
         mm2(1, 0)
+        cap_all(0)
+        quant_y(4)
+        scale_r(2, 1)
+        sub_u(3, 0)
+        mm1(3, 1)
+        floor_all(0)
+        group_e(2, 0)
+        group_e(2, 1)
         copy_d(1, 0)
         mm2(1, 1)
-        sub_u1(2)
-        sub_u0(3)
-        mm1(3, 1)
-        mul_w(2)
-        mul_w(3)
+        Ty(5, 0)
         copy_d(1, 1)
+        Gy(5, 0)
+        sub_u(3, 1)
+        turn_r(3, 0)
+        Ty(5, 1)
+        turn_r(3, 1)
         sub_d(1, 0)
         sub_d(1, 1)
-        sub_u1(3)
-        cap_all(1)
-        turn_r(2)
-        scale_r(2)
-        turn_e(2)
-        group_e(2)
-        group_r(2)
-        quant_e(2)
-        floor_all(1)
-        Ty(5, 0)
-        Ty(5, 1)
-        Gy(5, 0)
-        mm1(4, 0)
-        sub_u0(4)
         Gy(5, 1)
-        mm2(2, 0)
-        copy_d(2, 0)
-        sub_d(2, 0)
-        mm2(2, 1)
-        copy_d(2, 1)
-        turn_e(3)
-        turn_r(3)
-        sub_d(2, 1)
-        quant_y(5)
-        mm1(4, 1)
-        sub_u1(4)
-        group_e(3)
-        scale_r(3)
-        cap_all(2)
-        group_r(3)
-        quant_e(3)
-        Ty(6, 0)
-        Ty(6, 1)
-        mm1(5, 0)
-        mm2(3, 0)
-        mul_w(4)
-        turn_r(4)
-        mm2(3, 1)
-        floor_all(2)
-        Gy(6, 0)
-        Gy(6, 1)
-        turn_e(4)
-        sub_u0(5)
-        copy_d(3, 0)
-        sub_d(3, 0)
-        copy_d(3, 1)
-        sub_d(3, 1)
-        mm1(5, 1)
-        group_e(4)
-        quant_y(6)
-        sub_u1(5)
-        scale_r(4)
-        group_r(4)
-        quant_e(4)
         store_d(1)
-        Ty(7, 0)
-        Gy(7, 0)
-        Ty(7, 1)
-        Gy(7, 1)
+        quant_e(2)
+        mm1(4, 0)
+        scale_r(3, 0)
+        mm2(2, 0)
+        cap_all(1)
+        quant_y(5)
+        scale_r(3, 1)
+        sub_u(4, 0)
+        mm1(4, 1)
+        floor_all(1)
+        group_e(3, 0)
+        group_e(3, 1)
+        copy_d(2, 0)
+        mm2(2, 1)
+        Ty(6, 0)
+        copy_d(2, 1)
+        Gy(6, 0)
+        sub_u(4, 1)
+        turn_r(4, 0)
+        Ty(6, 1)
+        turn_r(4, 1)
+        sub_d(2, 0)
+        sub_d(2, 1)
+        Gy(6, 1)
         store_d(2)
+        quant_e(3)
+        mm1(5, 0)
+        scale_r(4, 0)
+        mm2(3, 0)
+        cap_all(2)
+        quant_y(6)
+        scale_r(4, 1)
+        sub_u(5, 0)
+        mm1(5, 1)
+        floor_all(2)
+        group_e(4, 0)
+        group_e(4, 1)
+        copy_d(3, 0)
+        mm2(3, 1)
+        Ty(7, 0)
+        copy_d(3, 1)
+        Gy(7, 0)
+        sub_u(5, 1)
+        turn_r(5, 0)
+        Ty(7, 1)
+        turn_r(5, 1)
+        sub_d(3, 0)
+        sub_d(3, 1)
+        Gy(7, 1)
         store_d(3)
-        mul_w(5)
+        quant_e(4)
         mm1(6, 0)
-        mm1(6, 1)
+        scale_r(5, 0)
         mm2(4, 0)
-        mm2(4, 1)
-        copy_d(4, 0)
-        copy_d(4, 1)
-        store_d(4)
-        turn_e(5)
-        turn_r(5)
-        group_e(5)
-        scale_r(5)
-        group_r(5)
         cap_all(3)
         quant_y(7)
+        scale_r(5, 1)
+        sub_u(6, 0)
+        mm1(6, 1)
         floor_all(3)
-        sub_u0(6)
-        sub_u1(6)
+        group_e(5, 0)
+        group_e(5, 1)
+        copy_d(4, 0)
+        mm2(4, 1)
+        copy_d(4, 1)
+        sub_u(6, 1)
+        turn_r(6, 0)
+        turn_r(6, 1)
         sub_d(4, 0)
         sub_d(4, 1)
+        store_d(4)
         quant_e(5)
-        mul_w(6)
         mm1(7, 0)
-        mm1(7, 1)
+        scale_r(6, 0)
         mm2(5, 0)
-        mm2(5, 1)
-        copy_d(5, 0)
-        copy_d(5, 1)
-        store_d(5)
-        turn_e(6)
-        turn_r(6)
-        group_e(6)
-        scale_r(6)
-        group_r(6)
         cap_all(4)
+        scale_r(6, 1)
+        sub_u(7, 0)
+        mm1(7, 1)
         floor_all(4)
-        sub_u0(7)
-        sub_u1(7)
+        group_e(6, 0)
+        group_e(6, 1)
+        copy_d(5, 0)
+        mm2(5, 1)
+        copy_d(5, 1)
+        sub_u(7, 1)
+        turn_r(7, 0)
+        turn_r(7, 1)
         sub_d(5, 0)
         sub_d(5, 1)
+        store_d(5)
         quant_e(6)
-        mul_w(7)
+        scale_r(7, 0)
         mm2(6, 0)
-        mm2(6, 1)
-        copy_d(6, 0)
-        copy_d(6, 1)
-        store_d(6)
-        turn_e(7)
-        turn_r(7)
-        group_e(7)
-        scale_r(7)
-        group_r(7)
         cap_all(5)
+        scale_r(7, 1)
         floor_all(5)
+        group_e(7, 0)
+        group_e(7, 1)
+        copy_d(6, 0)
+        mm2(6, 1)
+        copy_d(6, 1)
         sub_d(6, 0)
         sub_d(6, 1)
+        store_d(6)
         quant_e(7)
         mm2(7, 0)
-        mm2(7, 1)
-        copy_d(7, 0)
-        copy_d(7, 1)
-        store_d(7)
         cap_all(6)
         floor_all(6)
+        copy_d(7, 0)
+        mm2(7, 1)
+        copy_d(7, 1)
         sub_d(7, 0)
         sub_d(7, 1)
+        store_d(7)
         cap_all(7)
         floor_all(7)

from contextlib import ExitStack

import concourse.mybir as mybir
from concourse.masks import make_identity

M, K, N = 1024, 2048, 1024
FLOPS = 2 * M * K * N + 2 * M * N * N

F32 = mybir.dt.float32
BF16 = mybir.dt.bfloat16
I32 = mybir.dt.int32
U32 = mybir.dt.uint32
U8 = mybir.dt.uint8
E4M3 = mybir.dt.float8_e4m3fn_x4
E5M2 = mybir.dt.float8_e5m2_x4
E2M1 = mybir.dt.float4_e2m1fn_x4
ADD = mybir.AluOpType.add
SUB = mybir.AluOpType.subtract
MUL = mybir.AluOpType.mult
MIN = mybir.AluOpType.min
MAX = mybir.AluOpType.max
COPY = mybir.ActivationFunctionType.Copy

P = 128
PACK = 4
KG = K // 512
NG = N // 512
TILES = M // P
HALF = 512
QE = ""


def tile_lifted_disturbance_observer_s9_kernel(
    tc, y, pinv_words, pinv_scales, u, window, qfilter, command, limit, out_0, out_1
):
    nc = tc.nc
    with ExitStack() as ctx:
        keep = ctx.enter_context(tc.tile_pool(name="keep", bufs=1))
        rows = ctx.enter_context(tc.tile_pool(name="rows", bufs=TILES))
        work = ctx.enter_context(tc.tile_pool(name="work", bufs=3))
        deep = ctx.enter_context(tc.tile_pool(name="deep", bufs=3))
        ps_y = ctx.enter_context(tc.psum_pool(name="ps_y", bufs=2))
        ps_h = ctx.enter_context(tc.psum_pool(name="ps_h", bufs=2))
        ps_d = ctx.enter_context(tc.psum_pool(name="ps_d", bufs=2))
        ps_r = ctx.enter_context(tc.psum_pool(name="ps_r", bufs=2))
        ctx.enter_context(tc.manual_schedule())

        ident = keep.tile([P, P], F32, name="ident")
        ident_b = keep.tile([P, P], BF16, name="ident_b")
        vec = keep.tile([P, P], BF16, name="vec")
        vcol = keep.tile([P, 8], BF16, name="vcol")
        wcol_b = keep.tile([P, NG, PACK], BF16, name="wcol_b")
        wcol = keep.tile([P, NG, PACK], F32, name="wcol")
        warm = keep.tile([P, 1], F32, name="warm")
        lb = keep.tile([P, N], BF16, name="lb")
        nlb = keep.tile([P, N], BF16, name="nlb")
        pw = keep.tile([P, KG, 2 * N], U8, name="pw", align_bytes=64)
        pscale = keep.tile([P, KG, N], U8, name="pscale", align_bytes=64)
        q_raw = keep.tile([P, NG, PACK, N], BF16, name="q_raw")
        q_grp = keep.tile([P, NG, 2, HALF, PACK], BF16, name="q_grp", align_bytes=64)
        q_codes = keep.tile([P, NG, N], U32, name="q_codes", align_bytes=64)
        q_scale = keep.tile([P, NG, N], U8, name="q_scale", align_bytes=64)

        T = [dict() for i in range(TILES)]

        def rsl(i):
            return slice(i * P, (i + 1) * P)

        def load_y(i, parts=1):
            t = rows.tile([P, K], BF16, name="y_sb")
            T[i]["y"] = t
            w = K // parts
            for j in range(parts):
                nc.sync.dma_start(out=t[:, j * w : (j + 1) * w], in_=y[rsl(i), j * w : (j + 1) * w])

        def load_u(i):
            t = rows.tile([P, N], BF16, name="u_sb")
            T[i]["u"] = t
            nc.sync.dma_start(out=t[:], in_=u[rsl(i), :])

        def load_c(i):
            t = rows.tile([P, N], BF16, name="c_sb")
            T[i]["c"] = t
            nc.sync.dma_start(out=t[:], in_=command[rsl(i), :])

        def load_q(g):
            nc.sync.dma_start(
                out=q_raw[:, g, :, :],
                in_=qfilter[g * 512 : (g + 1) * 512, :].rearrange("(p j) n -> p j n", j=PACK),
            )

        def turn_y(i, b):
            words = T[i]["y"][:].bitcast(F32)
            bank = ps_y.tile([P, 2, 2, P], F32, name="yT", tag="yT")
            T[i]["yT", b] = bank
            for gg in range(2):
                g = 2 * b + gg
                for h in range(2):
                    nc.tensor.transpose(
                        bank[:, gg, h, :], words[:, 256 * g + h : 256 * (g + 1) : 2], ident[:]
                    )

        def group_y(i, b):
            if b == 0:
                grp = work.tile([P, KG, P, PACK], BF16, name="y_grp", align_bytes=64)
                T[i]["yg"] = grp
            wv = T[i]["yg"][:].rearrange("p g m t -> p (g m t)").bitcast(F32)
            nc.scalar.copy(
                out=wv[:, 512 * b : 512 * (b + 1)].rearrange("p (g m h) -> p g m h", g=2, h=2),
                in_=T[i]["yT", b][:].rearrange("p g h m -> p g m h"),
            )

        def quant_y(i):
            codes = deep.tile([P, KG * P], U32, name="y_codes", align_bytes=64)
            scale = deep.tile([P, KG * P], U8, name="y_scale", align_bytes=64)
            T[i]["yc"] = codes
            T[i]["ys"] = scale
            nc.vector.quantize_mx(
                out=codes[:].bitcast(E4M3), scales=scale[:],
                in_=T[i]["yg"][:].rearrange("p g m t -> p (g m t)"),
            )

        def mm1(i, n):
            acc = ps_h.tile([P, HALF], F32, name="h", tag="h")
            T[i]["h", n] = acc
            for g in range(KG):
                nc.tensor.matmul_mx(
                    out=acc[:],
                    lhsT=T[i]["yc"][:, g * P : (g + 1) * P].bitcast(E4M3),
                    lhsT_scale=T[i]["ys"][:, g * P : (g + 1) * P],
                    rhs=pw[:, g, n * N : (n + 1) * N].bitcast(E2M1),
                    rhs_scale=pscale[:, g, n * HALF : (n + 1) * HALF],
                    start=(g == 0),
                    stop=(g == KG - 1),
                )

        def sub_u(i, n):
            if n == 0:
                r = work.tile([P, NG, PACK, P], F32, name="r")
                T[i]["r"] = r
            c = slice(n * HALF, (n + 1) * HALF)
            nc.vector.tensor_tensor(
                out=T[i]["r"][:, n, :, :],
                in0=T[i]["h", n][:].rearrange("p (w t) -> p t w", t=PACK),
                in1=T[i]["u"][:, c].rearrange("p (w t) -> p t w", t=PACK),
                op=SUB,
            )

        def turn_r(i, n):
            bank = ps_r.tile([P, PACK, P], F32, name="rT", tag="rT")
            T[i]["rT", n] = bank
            for t in range(PACK):
                nc.tensor.transpose(bank[:, t, :], T[i]["r"][:, n, t, :], ident[:])

        def scale_r(i, n):
            if n == 0:
                e = work.tile([P, NG, PACK, P], BF16, name="e")
                T[i]["e"] = e
            for t in range(PACK):
                nc.scalar.activation(
                    out=T[i]["e"][:, n, t, :], in_=T[i]["rT", n][:, t, :], func=COPY, scale=wcol[:, n, t : t + 1]
                )

        def group_e(i, n):
            if n == 0:
                grp = work.tile([P, NG, P, PACK], BF16, name="e_grp", align_bytes=64)
                T[i]["eg"] = grp
            nc.scalar.copy(
                out=T[i]["eg"][:, n, :, :].rearrange("p (c k) t -> p c t k", k=4),
                in_=T[i]["e"][:, n, :, :].rearrange("p t (c k) -> p c t k", k=4),
            )

        def quant_e(i):
            codes = work.tile([P, NG * P], U32, name="e_codes", align_bytes=64)
            scale = work.tile([P, NG * P], U8, name="e_scale", align_bytes=64)
            T[i]["ec"] = codes
            T[i]["es"] = scale
            nc.vector.quantize_mx(
                out=codes[:].bitcast(E5M2), scales=scale[:],
                in_=T[i]["eg"][:].rearrange("p g m t -> p (g m t)"),
            )

        def mm2(i, n):
            acc = ps_d.tile([P, HALF], F32, name="d")
            T[i]["d", n] = acc
            for g in range(NG):
                nc.tensor.matmul_mx(
                    out=acc[:],
                    lhsT=T[i]["ec"][:, g * P : (g + 1) * P].bitcast(E5M2),
                    lhsT_scale=T[i]["es"][:, g * P : (g + 1) * P],
                    rhs=q_codes[:, g, n * HALF : (n + 1) * HALF].bitcast(E4M3),
                    rhs_scale=q_scale[:, g, n * HALF : (n + 1) * HALF],
                    start=(g == 0),
                    stop=(g == NG - 1),
                )

        def copy_d(i, n):
            if n == 0:
                t = deep.tile([P, N], F32, name="d_sb")
                T[i]["ds"] = t
            nc.scalar.copy(out=T[i]["ds"][:, n * HALF : (n + 1) * HALF], in_=T[i]["d", n][:])

        def store_d(i):
            nc.sync.dma_start(out=out_0[rsl(i), :], in_=T[i]["ds"][:])

        def sub_d(i, n):
            if n == 0:
                x = work.tile([P, N], F32, name="x")
                T[i]["x"] = x
            c = slice(n * HALF, (n + 1) * HALF)
            nc.vector.tensor_tensor(out=T[i]["x"][:, c], in0=T[i]["c"][:, c], in1=T[i]["d", n][:], op=SUB)

        def cap(i, c):
            nc.vector.tensor_tensor(out=T[i]["x"][:, c], in0=T[i]["x"][:, c], in1=lb[:, c], op=MIN)

        def floor_(i, c):
            if "v" not in T[i]:
                t = deep.tile([P, N], F32, name="v")
                T[i]["v"] = t
            nc.vector.tensor_tensor(out=T[i]["v"][:, c], in0=T[i]["x"][:, c], in1=nlb[:, c], op=MAX)

        def store_v(i, c):
            nc.sync.dma_start(out=out_1[rsl(i), c], in_=T[i]["v"][:, c])

        def group_q(n, g, eng):
            src = q_raw[:, g, :, n * HALF : (n + 1) * HALF].rearrange("p j (c k) -> p c j k", k=4)
            dst = q_grp[:, g, n, :, :].rearrange("p (c k) j -> p c j k", k=4)
            if eng == "S":
                nc.scalar.copy(out=dst, in_=src)
            elif eng == "G":
                nc.gpsimd.tensor_scalar(out=dst, in0=src, scalar1=1.0, scalar2=0.0, op0=MUL, op1=ADD)
            else:
                nc.vector.tensor_copy(out=dst, in_=src)

        def quant_q(n, g):
            c = slice(n * HALF, (n + 1) * HALF)
            nc.vector.quantize_mx(
                out=q_codes[:, g, c].bitcast(E4M3), scales=q_scale[:, g, c],
                in_=q_grp[:, g, n, :, :].rearrange("p c j -> p (c j)"),
            )

        def bcast(dst_ps, j0, count):
            for j in range(count):
                nc.tensor.transpose(
                    dst_ps[:, j * P : (j + 1) * P], vcol[:, j0 + j : j0 + j + 1].to_broadcast([P, P]), ident_b[:]
                )

        def cap_all(i):
            w = N if i < TILES - 1 else 256
            for c0 in range(0, N, w):
                cap(i, slice(c0, c0 + w))

        def floor_all(i):
            w = N if i < TILES - 1 else 256
            for c0 in range(0, N, w):
                floor_(i, slice(c0, c0 + w))
                store_v(i, slice(c0, c0 + w))

        def prep():
            nc.vector.tensor_copy(out=wcol[:], in_=wcol_b[:])
            vT = ps_r.tile([P, P], BF16, name="vT", tag="rT")
            nc.tensor.transpose(vT[:], vec[:], ident_b[:])
            nc.scalar.copy(out=vcol[:], in_=vT[:, 0:8])

        def spread_l():
            lB = ps_d.tile([P, N], BF16, name="lB", tag="d")
            bcast(lB, 0, 8)
            nc.scalar.copy(out=lb[:], in_=lB[:])
            nc.gpsimd.tensor_scalar(out=nlb[:], in0=lb[:], scalar1=-1.0, scalar2=0.0, op0=MUL, op1=ADD)

        def load_p(g):
            nc.sync.dma_start(out=pw[:, g, :].bitcast(I32), in_=pinv_words[g].bitcast(I32))

        def load_s():
            for Q in range(4):
                nc.sync.dma_start(
                    out=ps32[32 * Q : 32 * Q + 4, :].rearrange("q (g n) -> q g n", g=KG),
                    in_=pinv_scales[:, 4 * Q : 4 * Q + 4, :].bitcast(I32).rearrange("g q n -> q g n"),
                )

        ps32 = pscale[:].rearrange("p g n -> p (g n)").bitcast(I32)
        nc.vector.memset(warm[:], 0.0)
        nc.vector.memset(ps32, 0)
        nc.vector.memset(vec[:], 0.0)
        nc.scalar.copy(out=warm[:], in_=warm[:])
        make_identity(nc, ident[:])
        make_identity(nc, ident_b[:])
        load_y(0)
        load_s()
        load_p(0)
        load_p(1)
        load_p(2)
        load_p(3)
        nc.scalar.dma_start(out=vec[0:8, :], in_=limit.rearrange("(a b) -> a b", b=P))
        nc.scalar.dma_start(out=wcol_b[:], in_=window.rearrange("(g p t) -> p g t", p=P, t=PACK))
        load_u(0)
        load_y(1)
        load_u(1)
        load_q(0)
        load_y(2)
        load_q(1)
        load_u(2)
        load_c(0)
        load_y(3)
        load_u(3)
        load_c(1)
        load_y(4)
        load_u(4)
        load_c(2)
        load_y(5)
        load_u(5)
        load_c(3)
        load_y(6)
        load_u(6)
        load_c(4)
        load_y(7)
        load_u(7)
        load_c(5)
        load_c(6)
        load_c(7)

        def Ty(i, b):
            turn_y(i, b)

        def Gy(i, b):
            group_y(i, b)

        Ty(0, 0)
        Gy(0, 0)
        Ty(0, 1)
        Gy(0, 1)
        quant_y(0)
        prep()
        spread_l()
        mm1(0, 0)
        sub_u(0, 0)
        Ty(1, 0)
        Ty(1, 1)
        Gy(1, 0)
        group_q(1, 0, "G")
        turn_r(0, 0)
        Gy(1, 1)
        quant_y(1)
        mm1(0, 1)
        mm1(1, 0)
        Ty(2, 0)
        group_q(0, 0, "S")
        Ty(2, 1)
        sub_u(0, 1)
        sub_u(1, 0)
        scale_r(0, 0)
        Gy(2, 0)
        turn_r(0, 1)
        scale_r(0, 1)
        quant_q(0, 0)
        mm1(1, 1)
        group_q(1, 1, "V")
        sub_u(1, 1)
        Gy(2, 1)
        turn_r(1, 0)
        turn_r(1, 1)
        group_e(0, 0)
        group_e(0, 1)
        Ty(3, 0)
        quant_y(2)
        group_q(0, 1, "V")
        scale_r(1, 0)
        quant_e(0)
        quant_q(1, 0)
        mm1(2, 0)
        quant_q(0, 1)
        Ty(3, 1)
        Gy(3, 0)
        Ty(4, 0)
        quant_q(1, 1)
        sub_u(2, 0)
        mm2(0, 0)
        sub_d(0, 0)
        mm2(0, 1)
        sub_d(0, 1)
        scale_r(1, 1)
        Gy(3, 1)
        quant_y(3)
        mm1(2, 1)
        group_e(1, 0)
        group_e(1, 1)
        copy_d(0, 0)
        copy_d(0, 1)
        Gy(4, 0)
        sub_u(2, 1)
        turn_r(2, 0)
        Ty(4, 1)
        turn_r(2, 1)
        Gy(4, 1)
        store_d(0)
        quant_e(1)
        mm1(3, 0)
        scale_r(2, 0)
        mm2(1, 0)
        cap_all(0)
        quant_y(4)
        scale_r(2, 1)
        sub_u(3, 0)
        mm1(3, 1)
        floor_all(0)
        group_e(2, 0)
        group_e(2, 1)
        copy_d(1, 0)
        mm2(1, 1)
        Ty(5, 0)
        copy_d(1, 1)
        Gy(5, 0)
        sub_u(3, 1)
        turn_r(3, 0)
        Ty(5, 1)
        turn_r(3, 1)
        sub_d(1, 0)
        sub_d(1, 1)
        Gy(5, 1)
        store_d(1)
        quant_e(2)
        mm1(4, 0)
        scale_r(3, 0)
        mm2(2, 0)
        cap_all(1)
        quant_y(5)
        scale_r(3, 1)
        sub_u(4, 0)
        mm1(4, 1)
        floor_all(1)
        group_e(3, 0)
        group_e(3, 1)
        copy_d(2, 0)
        mm2(2, 1)
        Ty(6, 0)
        copy_d(2, 1)
        Gy(6, 0)
        sub_u(4, 1)
        turn_r(4, 0)
        Ty(6, 1)
        turn_r(4, 1)
        sub_d(2, 0)
        sub_d(2, 1)
        Gy(6, 1)
        store_d(2)
        quant_e(3)
        mm1(5, 0)
        scale_r(4, 0)
        mm2(3, 0)
        cap_all(2)
        quant_y(6)
        scale_r(4, 1)
        sub_u(5, 0)
        mm1(5, 1)
        floor_all(2)
        group_e(4, 0)
        group_e(4, 1)
        copy_d(3, 0)
        mm2(3, 1)
        Ty(7, 0)
        copy_d(3, 1)
        Gy(7, 0)
        sub_u(5, 1)
        turn_r(5, 0)
        Ty(7, 1)
        turn_r(5, 1)
        sub_d(3, 0)
        sub_d(3, 1)
        Gy(7, 1)
        store_d(3)
        quant_e(4)
        mm1(6, 0)
        scale_r(5, 0)
        mm2(4, 0)
        cap_all(3)
        quant_y(7)
        scale_r(5, 1)
        sub_u(6, 0)
        mm1(6, 1)
        floor_all(3)
        group_e(5, 0)
        group_e(5, 1)
        copy_d(4, 0)
        mm2(4, 1)
        copy_d(4, 1)
        sub_u(6, 1)
        turn_r(6, 0)
        turn_r(6, 1)
        sub_d(4, 0)
        sub_d(4, 1)
        store_d(4)
        quant_e(5)
        mm1(7, 0)
        scale_r(6, 0)
        mm2(5, 0)
        cap_all(4)
        scale_r(6, 1)
        sub_u(7, 0)
        mm1(7, 1)
        floor_all(4)
        group_e(6, 0)
        group_e(6, 1)
        copy_d(5, 0)
        mm2(5, 1)
        copy_d(5, 1)
        sub_u(7, 1)
        turn_r(7, 0)
        turn_r(7, 1)
        sub_d(5, 0)
        sub_d(5, 1)
        store_d(5)
        quant_e(6)
        scale_r(7, 0)
        mm2(6, 0)
        cap_all(5)
        scale_r(7, 1)
        floor_all(5)
        group_e(7, 0)
        group_e(7, 1)
        copy_d(6, 0)
        mm2(6, 1)
        copy_d(6, 1)
        sub_d(6, 0)
        sub_d(6, 1)
        store_d(6)
        quant_e(7)
        mm2(7, 0)
        cap_all(6)
        floor_all(6)
        copy_d(7, 0)
        mm2(7, 1)
        copy_d(7, 1)
        sub_d(7, 0)
        sub_d(7, 1)
        store_d(7)
        cap_all(7)
        floor_all(7)
